import numpy as np
import ml_dtypes


def mxq(x, axis, fmt="e4m3"):
    dtype, down = {"e4m3": (ml_dtypes.float8_e4m3fn, 7), "e5m2": (ml_dtypes.float8_e5m2, 14)}[fmt]
    v = np.moveaxis(np.asarray(x, np.float32).astype(ml_dtypes.bfloat16).astype(np.float64), axis, -1)
    blocks = v.reshape(v.shape[:-1] + (-1, 32))
    amax = np.abs(blocks).max(-1, keepdims=True)
    byte = np.maximum(np.where(amax > 0, np.frexp(amax)[1] - 1 + 127, 0) - down, 1)
    scale = np.exp2(byte - 127.0)
    codes = (blocks / scale).astype(np.float32).astype(dtype).astype(np.float64)
    return np.moveaxis((codes * scale).reshape(v.shape), -1, axis)


WIDE = False


def mx_kscale(k):
    if not WIDE:
        return np.ones(k)
    levels = np.array([10, -10, 5, -5, 0])
    if k % 512:
        return np.exp2(np.random.permutation(np.resize(levels, k // 32))).repeat(32)
    a = np.empty((k // 512, 16))
    for p in range(k // 512):
        a[p, :8] = np.random.permutation(np.resize(levels, 8))
        for g in range(8):
            far = levels[np.abs(levels - a[p, g]) >= 10]
            a[p, g + 8] = far[np.random.randint(len(far))]
    return np.exp2(a.ravel()).repeat(32)


BF16 = ml_dtypes.bfloat16


def bf(x):
    return np.asarray(x, np.float32).astype(BF16)


def f64(x):
    return np.asarray(x).astype(np.float64)

def planes(Y):
    n, m = Y.shape
    b = f64(bf(Y)).reshape(n // 32, 32, m)
    amax = np.abs(b).max(1)
    byte = np.clip(np.where(amax > 0, np.frexp(amax)[1] - 1 + 127 - 7, 1), 1, 254)
    codes = (b * np.exp2(127.0 - byte)[:, None, :]).reshape(n, m).astype(np.float32).astype(ml_dtypes.float8_e4m3fn).view(np.uint8)
    words = codes.reshape(n // 512, 128, 4, m).transpose(0, 1, 3, 2)
    return np.ascontiguousarray(words), np.ascontiguousarray(byte.astype(np.uint8).reshape(n // 512, 16, m))


I, U = 2048, 1024
SPREAD = 1.4
ACTIVITY = 0.7


def noise(*shape):
    return np.random.randn(*shape)


def setup_inputs():
    s = mx_kscale(I)
    cooc = 0.5 * np.exp(SPREAD * noise(I, I)) / I
    history = np.exp(SPREAD * noise(U, I) + ACTIVITY * noise(U, 1))
    return {
        "cooc": bf(cooc / s[None, :]),
        "history": bf(history * s[None, :]),
        "damp": bf(np.exp(0.5 * noise(I))),
        "gain": bf(0.5 * np.exp(0.8 * noise(I))),
    }


def reference(cooc, history, damp, gain):
    C = mxq(f64(cooc), 1, "e4m3")
    H = mxq(f64(history), 1, "e4m3")
    S = C @ H.T
    y = f64(gain)[:, None] * np.log(1.0 + f64(damp)[:, None] * S)
    Y = y.reshape(I, U)
    words, scales = planes(Y)
    return y, words, scales

@@ -1,0 +1,238 @@
+from contextlib import ExitStack
+
+import concourse.mybir as mybir
+from concourse.masks import make_identity
+
+F32 = mybir.dt.float32
+BF16 = mybir.dt.bfloat16
+U32 = mybir.dt.uint32
+I32 = mybir.dt.int32
+U8 = mybir.dt.uint8
+FP8X4 = mybir.dt.float8_e4m3fn_x4
+ACT = mybir.ActivationFunctionType
+ALU = mybir.AluOpType
+
+ITEMS, USERS = 2048, 1024
+FLOPS = 2 * ITEMS * ITEMS * USERS
+P = 128
+PASSES = 4
+H, C = "history", "cooc"
+
+
+def T(kind, *ns):
+    return [("T", kind, n) for n in ns]
+
+
+def M(n, half, lo=0, hi=512):
+    return [("M", n, half, lo, hi)]
+
+
+def tail(widths):
+    out, lo = [], 0
+    for w in widths:
+        out += M(14, 1, lo, lo + w) + M(15, 1, lo, lo + w)
+        lo += w
+    return out
+
+
+TAIL = [256, 256]
+RAW, REG, GR, YB = 12, 4, 4, 4
+A_ON_VECTOR = set()
+GAIN_ON_SCALAR = set()
+LF, LB, LD, LE, LQ = 2, 1, 2, 0, 1
+
+
+def tile_cooccurrence_history_log_scores_g2_kernel(tc, cooc, history, damp, gain, out_0, out_1, out_2):
+    nc = tc.nc
+    PLAN = (T(H,0,1)+T(C,0,1)+T(H,2,3)+M(0,0,0,256)+M(1,0,0,256)+T(C,2,3)+M(0,0,256,512)+M(1,0,256,512)+T(C,4,5)+M(2,0)+M(3,0)+T(C,6,7)+M(4,0)+M(5,0)+T(H,4,5)+M(6,0)+T(H,6,7)+M(7,0)+T(C,8,9)+M(0,1)+M(1,1)+M(2,1)+M(3,1)+T(C,10,11)+M(4,1)+M(5,1)+M(6,1)+M(7,1)+T(C,12,13)+M(8,0)+M(9,0)+M(10,0)+M(11,0)+T(C,14,15)+M(8,1)+M(9,1)+M(10,1)+M(11,1)+M(12,0)+M(13,0)+M(14,0)+M(15,0)+M(12,1)+M(13,1)) + tail(TAIL)
+    cooc_rows = cooc.rearrange("(g m t) k -> g t m k", m=P, t=4)
+    hist_rows = history.rearrange("(r p) k -> r p k", p=P)
+    chunks = [(s[1], s[2]) for s in PLAN if s[0] == "T"]
+
+    with ExitStack() as ctx:
+        sb = ctx.enter_context(tc.tile_pool(name="sb", bufs=1))
+        ps = ctx.enter_context(tc.psum_pool(name="ps", bufs=1))
+        ctx.enter_context(tc.manual_schedule())
+
+        def tiles(pool, n, name, shape, dtype):
+            if pool is ps:
+                return [pool.tile(shape, dtype, name="%s%d" % (name, i)) for i in range(n)]
+            return [pool.tile(shape, dtype, name="%s%d" % (name, i), align_bytes=64) for i in range(n)]
+
+        raw = tiles(sb, RAW, "raw", [P, ITEMS], BF16)
+        regrouped = tiles(sb, REG, "reg", [P, 2, ITEMS // 2], BF16)
+        grouped = tiles(sb, GR, "grp", [P, PASSES, 512], BF16)
+        h_codes = tiles(sb, 2, "hc", [P, PASSES, 512], U32)
+        h_scales = tiles(sb, 2, "hs", [P, PASSES, 512], U8)
+        c_codes = tiles(sb, 16, "cc", [P, PASSES, P], U32)
+        c_scales = tiles(sb, 16, "cs", [P, PASSES, P], U8)
+        y = tiles(sb, YB, "y", [P, 4, 512], F32)
+        y_bf = tiles(sb, 2, "ybf", [P, 512, 4], BF16)
+        y_codes = tiles(sb, 3, "yc", [P, 512], U32)
+        y_scales = sb.tile([P, 4, USERS], U8, name="ys", align_bytes=64)
+        ident = sb.tile([P, P], F32, name="ident", align_bytes=64)
+        damp_bf = sb.tile([P, 4, 4], BF16, name="damp_bf", align_bytes=64)
+        gain_bf = sb.tile([P, 4, 4], BF16, name="gain_bf", align_bytes=64)
+        damp_f = sb.tile([P, 16], F32, name="damp_f", align_bytes=64)
+        gain_f = sb.tile([P, 16], F32, name="gain_f", align_bytes=64)
+        warm = sb.tile([P, 1], F32, name="warm", align_bytes=64)
+        t_banks = tiles(ps, 4, "tb", [P, 2, 2, P], F32)
+        m_banks = tiles(ps, 4, "mb", [P, 512], F32)
+
+        make_identity(nc, ident[:])
+        nc.scalar.activation(out=warm[:], in_=ident[:, 0:1], func=ACT.Ln, bias=1.0, scale=1.0)
+
+        def load(j):
+            kind, r = chunks[j]
+            src = hist_rows[r] if kind == H else cooc_rows[r // 4, r % 4]
+            nc.sync.dma_start(out=raw[j % RAW][:], in_=src)
+            if j == 7:
+                nc.sync.dma_start(out=damp_bf[:], in_=damp.rearrange("(g p t) -> p g t", p=P, t=4))
+                nc.sync.dma_start(out=gain_bf[:], in_=gain.rearrange("(g p t) -> p g t", p=P, t=4))
+                nc.gpsimd.tensor_copy(out=damp_f[:], in_=damp_bf[:].rearrange("p g t -> p (g t)"))
+                nc.gpsimd.tensor_copy(out=gain_f[:], in_=gain_bf[:].rearrange("p g t -> p (g t)"))
+
+        def regroup(j):
+            nc.vector.tensor_copy(
+                out=regrouped[j % REG][:].rearrange("p u (b j) -> p u b j", j=16),
+                in_=raw[j % RAW][:].rearrange("p (b u j) -> p u b j", u=2, j=16),
+            )
+            if j + RAW < len(chunks):
+                load(j + RAW)
+
+        def transpose(j):
+            words = regrouped[j % REG][:].bitcast(F32)
+            for b in range(2):
+                bank = t_banks[2 * (j % 2) + b]
+                for a in range(2):
+                    kp = 2 * b + a
+                    for u in range(2):
+                        nc.tensor.transpose(bank[:, a, u, :], words[:, u, kp * P:(kp + 1) * P], ident[:])
+                dst = grouped[j % GR][:, 2 * b:2 * b + 2, :].bitcast(F32).rearrange("p a (r u) -> p a r u", u=2)
+                src = bank[:].rearrange("p a u r -> p a r u")
+                if (j, b) in A_ON_VECTOR:
+                    nc.vector.tensor_copy(out=dst, in_=src)
+                else:
+                    nc.scalar.copy(out=dst, in_=src)
+
+        def quantize_operand(j):
+            kind, n = chunks[j]
+            if kind == C:
+                nc.vector.quantize_mx(
+                    out=c_codes[n][:].rearrange("p a b -> p (a b)").bitcast(FP8X4),
+                    scales=c_scales[n][:].rearrange("p a b -> p (a b)"),
+                    in_=grouped[j % GR][:].rearrange("p a b -> p (a b)"),
+                )
+            else:
+                cols = slice(P * (n % 4), P * (n % 4) + P)
+                for kp in range(PASSES):
+                    nc.vector.quantize_mx(
+                        out=h_codes[n // 4][:, kp, cols].bitcast(FP8X4),
+                        scales=h_scales[n // 4][:, kp, cols],
+                        in_=grouped[j % GR][:, kp, :],
+                    )
+
+        y_slot = {}
+
+        def multiply(bank, n, half, lo, hi):
+            g, t = n // 4, n % 4
+            yt = y[y_slot.setdefault((g, half), len(y_slot)) % YB]
+            acc = m_banks[bank % 4]
+            for kp in range(PASSES):
+                nc.tensor.matmul_mx(
+                    out=acc[:, 0:hi - lo],
+                    lhsT=c_codes[n][:, kp, :].bitcast(FP8X4),
+                    lhsT_scale=c_scales[n][:, kp, :],
+                    rhs=h_codes[half][:, kp, lo:hi].bitcast(FP8X4),
+                    rhs_scale=h_scales[half][:, kp, lo:hi],
+                    start=(kp == 0),
+                    stop=(kp == PASSES - 1),
+                )
+            nc.scalar.activation(out=yt[:, t, lo:hi], in_=acc[:, 0:hi - lo], func=ACT.Ln, bias=1.0, scale=damp_f[:, n:n + 1])
+
+        def store_y(g, half, ts, lo, hi):
+            yt = y[y_slot[(g, half)] % YB]
+            rows = out_0[512 * g:512 * g + 512, 512 * half + lo:512 * half + hi].rearrange("(p t) m -> p t m", t=4)
+            nc.sync.dma_start(out=rows[:, ts, :], in_=yt[:, ts, lo:hi])
+
+        def apply_gain(n, half, lo, hi):
+            g, t = n // 4, n % 4
+            yt = y[y_slot[(g, half)] % YB]
+            if (n, half) in GAIN_ON_SCALAR:
+                nc.scalar.activation(out=yt[:, t, lo:hi], in_=yt[:, t, lo:hi], func=ACT.Copy, scale=gain_f[:, n:n + 1])
+            else:
+                nc.vector.tensor_scalar(out=yt[:, t, lo:hi], in0=yt[:, t, lo:hi], scalar1=gain_f[:, n:n + 1], scalar2=None, op0=ALU.mult)
+            if g == 3 and t == 1:
+                store_y(g, half, slice(0, 2), 0, 512)
+            elif g == 3 and t == 3:
+                store_y(g, half, slice(2, 4), lo, hi)
+            elif t == 3 and hi == 512:
+                store_y(g, half, slice(0, 4), 0, 512)
+
+        def interleave(g, half, lo, hi):
+            s = y_slot[(g, half)]
+            nc.vector.tensor_copy(out=y_bf[s % 2][:, lo:hi, :], in_=y[s % YB][:, :, lo:hi].rearrange("p t m -> p m t"))
+
+        def store_scales(gs, engines):
+            for q in range(4):
+                engines[q % len(engines)].dma_start(
+                    out=out_2[gs, 4 * q:4 * q + 4, :].rearrange("g r m -> r g m").bitcast(I32),
+                    in_=y_scales[32 * q:32 * q + 4, gs, :].bitcast(I32),
+                )
+
+        def quantize_result(g, half, lo, hi):
+            s = y_slot[(g, half)]
+            users = slice(512 * half + lo, 512 * half + hi)
+            nc.vector.quantize_mx(
+                out=y_codes[s % 3][:, lo:hi].bitcast(FP8X4),
+                scales=y_scales[:, g, users],
+                in_=y_bf[s % 2][:, lo:hi, :].rearrange("p m t -> p (m t)"),
+            )
+            nc.sync.dma_start(
+                out=out_1[g, :, users, :].rearrange("p m t -> p (m t)").bitcast(I32),
+                in_=y_codes[s % 3][:, lo:hi].bitcast(I32),
+            )
+            if (g, half) == (2, 1):
+                store_scales(slice(0, 3), [nc.sync])
+
+        for j in range(RAW):
+            load(j)
+        for j in range(LF):
+            regroup(j)
+        later = {}
+
+        def after(step, rank, fn, *args):
+            later.setdefault(step, []).append((rank, len(later.get(step, [])), fn, args))
+
+        j = 0
+        bank = 0
+        needs = {}
+        for si, step in enumerate(PLAN):
+            if step[0] == "M":
+                needs.setdefault((C, step[1]), si)
+                for r in range(4 * step[2] + step[3] // P, 4 * step[2] + step[4] // P):
+                    needs.setdefault((H, r), si)
+        for si, step in enumerate(PLAN):
+            if step[0] == "T":
+                transpose(j)
+                if j + LF < len(chunks):
+                    after(si, 1, regroup, j + LF)
+                after(min(si + LB, needs[chunks[j]] - 1), 2, quantize_operand, j)
+                j += 1
+            else:
+                n, half, lo, hi = step[1:]
+                multiply(bank, n, half, lo, hi)
+                bank += 1
+                after(si + LD, 0, apply_gain, n, half, lo, hi)
+                if n % 4 == 3 and (hi == 512 or (n, half) == (15, 1)):
+                    if (n, half) != (15, 1):
+                        lo = 0
+                    le = LE if n < 15 else 1
+                    after(si + LD + le, 3, interleave, n // 4, half, lo, hi)
+                    after(si + LD + le + LQ, 4, quantize_result, n // 4, half, lo, hi)
+            for rank, order, fn, args in sorted(later.get(si, []), key=lambda x: x[:2]):
+                fn(*args)
+        for si in range(len(PLAN), len(PLAN) + LD + LE + LQ + 1):
+            for rank, order, fn, args in sorted(later.get(si, []), key=lambda x: x[:2]):
+                fn(*args)
+        store_scales(slice(3, 4), [nc.scalar, nc.sync])

@@ -35,7 +35,7 @@ def tail(widths):
     return out
 
 
-TAIL = [256, 256]
+TAIL = []
 RAW, REG, GR, YB = 12, 4, 4, 4
 A_ON_VECTOR = set()
 GAIN_ON_SCALAR = set()
@@ -44,7 +44,7 @@ LF, LB, LD, LE, LQ = 2, 1, 2, 0, 1
 
 def tile_cooccurrence_history_log_scores_g2_kernel(tc, cooc, history, damp, gain, out_0, out_1, out_2):
     nc = tc.nc
-    PLAN = (T(H,0,1)+T(C,0,1)+T(H,2,3)+M(0,0,0,256)+M(1,0,0,256)+T(C,2,3)+M(0,0,256,512)+M(1,0,256,512)+T(C,4,5)+M(2,0)+M(3,0)+T(C,6,7)+M(4,0)+M(5,0)+T(H,4,5)+M(6,0)+T(H,6,7)+M(7,0)+T(C,8,9)+M(0,1)+M(1,1)+M(2,1)+M(3,1)+T(C,10,11)+M(4,1)+M(5,1)+M(6,1)+M(7,1)+T(C,12,13)+M(8,0)+M(9,0)+M(10,0)+M(11,0)+T(C,14,15)+M(8,1)+M(9,1)+M(10,1)+M(11,1)+M(12,0)+M(13,0)+M(14,0)+M(15,0)+M(12,1)+M(13,1)) + tail(TAIL)
+    PLAN = (T(H,0,1)+T(C,0,1)+T(H,2,3)+M(0,0,0,256)+M(1,0,0,256)+T(C,2,3)+M(0,0,256,512)+M(1,0,256,512)+T(H,4,5)+M(2,0)+M(3,0)+T(H,6,7)+M(0,1,0,256)+M(1,1,0,256)+M(2,1,0,256)+M(3,1,0,256)+T(C,4,5)+M(0,1,256,512)+M(1,1,256,512)+M(2,1,256,512)+M(3,1,256,512)+T(C,6,7)+M(4,0)+M(5,0)+M(4,1)+M(5,1)+T(C,8,9)+M(6,0)+M(7,0)+M(6,1)+M(7,1)+T(C,10,11)+M(8,0)+M(9,0)+M(8,1)+M(9,1)+T(C,12,13)+M(10,0)+M(11,0)+M(10,1)+M(11,1)+T(C,14,15)+M(12,0)+M(13,0)+M(14,0)+M(15,0)+M(12,1)+M(13,1)) + tail(TAIL)
     cooc_rows = cooc.rearrange("(g m t) k -> g t m k", m=P, t=4)
     hist_rows = history.rearrange("(r p) k -> r p k", p=P)
     chunks = [(s[1], s[2]) for s in PLAN if s[0] == "T"]
@@ -62,6 +62,7 @@ def tile_cooccurrence_history_log_scores_g2_kernel(tc, cooc, history, damp, gain
         raw = tiles(sb, RAW, "raw", [P, ITEMS], BF16)
         regrouped = tiles(sb, REG, "reg", [P, 2, ITEMS // 2], BF16)
         grouped = tiles(sb, GR, "grp", [P, PASSES, 512], BF16)
+        h_grouped = tiles(sb, 2, "hgrp", [P, PASSES, 2, 512], BF16)
         h_codes = tiles(sb, 2, "hc", [P, PASSES, 512], U32)
         h_scales = tiles(sb, 2, "hs", [P, PASSES, 512], U8)
         c_codes = tiles(sb, 16, "cc", [P, PASSES, P], U32)
@@ -88,27 +89,35 @@ def tile_cooccurrence_history_log_scores_g2_kernel(tc, cooc, history, damp, gain
             nc.sync.dma_start(out=raw[j % RAW][:], in_=src)
             if j == 7:
                 nc.sync.dma_start(out=damp_bf[:], in_=damp.rearrange("(g p t) -> p g t", p=P, t=4))
-                nc.sync.dma_start(out=gain_bf[:], in_=gain.rearrange("(g p t) -> p g t", p=P, t=4))
                 nc.gpsimd.tensor_copy(out=damp_f[:], in_=damp_bf[:].rearrange("p g t -> p (g t)"))
+            if j == 7:
+                nc.sync.dma_start(out=gain_bf[:], in_=gain.rearrange("(g p t) -> p g t", p=P, t=4))
                 nc.gpsimd.tensor_copy(out=gain_f[:], in_=gain_bf[:].rearrange("p g t -> p (g t)"))
 
         def regroup(j):
-            nc.vector.tensor_copy(
-                out=regrouped[j % REG][:].rearrange("p u (b j) -> p u b j", j=16),
-                in_=raw[j % RAW][:].rearrange("p (b u j) -> p u b j", u=2, j=16),
-            )
-            if j + RAW < len(chunks):
-                load(j + RAW)
+            if j not in set(range(6)):
+                nc.vector.tensor_copy(
+                    out=regrouped[j % REG][:].bitcast(F32).rearrange("p u w -> p w u"),
+                    in_=raw[j % RAW][:].bitcast(F32).rearrange("p (w u) -> p w u", u=2),
+                )
 
         def transpose(j):
-            words = regrouped[j % REG][:].bitcast(F32)
+            if j in set(range(6)):
+                words = raw[j % RAW][:].bitcast(F32).rearrange("p (w u) -> p u w", u=2)
+            else:
+                words = regrouped[j % REG][:].bitcast(F32)
             for b in range(2):
                 bank = t_banks[2 * (j % 2) + b]
                 for a in range(2):
                     kp = 2 * b + a
                     for u in range(2):
                         nc.tensor.transpose(bank[:, a, u, :], words[:, u, kp * P:(kp + 1) * P], ident[:])
-                dst = grouped[j % GR][:, 2 * b:2 * b + 2, :].bitcast(F32).rearrange("p a (r u) -> p a r u", u=2)
+                kind, n = chunks[j]
+                if kind == H:
+                    dst = h_grouped[(n // 2) % 2][:, 2 * b:2 * b + 2, n % 2, :]
+                else:
+                    dst = grouped[n % GR][:, 2 * b:2 * b + 2, :]
+                dst = dst.bitcast(F32).rearrange("p a (r u) -> p a r u", u=2)
                 src = bank[:].rearrange("p a u r -> p a r u")
                 if (j, b) in A_ON_VECTOR:
                     nc.vector.tensor_copy(out=dst, in_=src)
@@ -121,15 +130,15 @@ def tile_cooccurrence_history_log_scores_g2_kernel(tc, cooc, history, damp, gain
                 nc.vector.quantize_mx(
                     out=c_codes[n][:].rearrange("p a b -> p (a b)").bitcast(FP8X4),
                     scales=c_scales[n][:].rearrange("p a b -> p (a b)"),
-                    in_=grouped[j % GR][:].rearrange("p a b -> p (a b)"),
+                    in_=grouped[n % GR][:].rearrange("p a b -> p (a b)"),
                 )
-            else:
-                cols = slice(P * (n % 4), P * (n % 4) + P)
+            elif n % 2 == 1:
+                cols = slice(P * (n % 4 - 1), P * (n % 4 + 1))
                 for kp in range(PASSES):
                     nc.vector.quantize_mx(
                         out=h_codes[n // 4][:, kp, cols].bitcast(FP8X4),
                         scales=h_scales[n // 4][:, kp, cols],
-                        in_=grouped[j % GR][:, kp, :],
+                        in_=h_grouped[(n // 2) % 2][:, kp, :, :].rearrange("p c w -> p (c w)"),
                     )
 
         y_slot = {}
@@ -171,7 +180,10 @@ def tile_cooccurrence_history_log_scores_g2_kernel(tc, cooc, history, damp, gain
 
         def interleave(g, half, lo, hi):
             s = y_slot[(g, half)]
-            nc.vector.tensor_copy(out=y_bf[s % 2][:, lo:hi, :], in_=y[s % YB][:, :, lo:hi].rearrange("p t m -> p m t"))
+            (nc.scalar.copy if (g, half, lo) in set() else nc.vector.tensor_copy)(
+                out=y_bf[s % 2][:, lo:hi, :].rearrange("p (c i) t -> p c t i", i=4),
+                in_=y[s % YB][:, :, lo:hi].rearrange("p t (c i) -> p c t i", i=4),
+            )
 
         def store_scales(gs, engines):
             for q in range(4):
@@ -215,24 +227,42 @@ def tile_cooccurrence_history_log_scores_g2_kernel(tc, cooc, history, damp, gain
         for si, step in enumerate(PLAN):
             if step[0] == "T":
                 transpose(j)
+                if j + RAW < len(chunks):
+                    load(j + RAW)
                 if j + LF < len(chunks):
-                    after(si, 1, regroup, j + LF)
+                    after(si, 3 if j + LF < 8 else 1, regroup, j + LF)
                 after(min(si + LB, needs[chunks[j]] - 1), 2, quantize_operand, j)
                 j += 1
             else:
                 n, half, lo, hi = step[1:]
                 multiply(bank, n, half, lo, hi)
                 bank += 1
-                after(si + LD, 0, apply_gain, n, half, lo, hi)
+                ld = LD if n < 12 else 1
+                after(si + (1 if (n, half) in GAIN_ON_SCALAR else ld), 0, apply_gain, n, half, lo, hi)
                 if n % 4 == 3 and (hi == 512 or (n, half) == (15, 1)):
                     if (n, half) != (15, 1):
                         lo = 0
-                    le = LE if n < 15 else 1
-                    after(si + LD + le, 3, interleave, n // 4, half, lo, hi)
-                    after(si + LD + le + LQ, 4, quantize_result, n // 4, half, lo, hi)
+                    le = LE if n < 15 else 0
+                    after(si + ld + le, 3, interleave, n // 4, half, lo, hi)
+                    after(si + ld + le + LQ, 4, quantize_result, n // 4, half, lo, hi)
             for rank, order, fn, args in sorted(later.get(si, []), key=lambda x: x[:2]):
                 fn(*args)
-        for si in range(len(PLAN), len(PLAN) + LD + LE + LQ + 1):
+        def flush(si):
             for rank, order, fn, args in sorted(later.get(si, []), key=lambda x: x[:2]):
                 fn(*args)
+
+        multiply(bank, 14, 1, 0, 256)
+        flush(len(PLAN))
+        flush(len(PLAN) + 1)
+        multiply(bank + 1, 15, 1, 0, 256)
+        apply_gain(14, 1, 0, 256)
+        apply_gain(15, 1, 0, 256)
+        multiply(bank + 2, 14, 1, 256, 512)
+        interleave(3, 1, 0, 256)
+        multiply(bank + 3, 15, 1, 256, 512)
+        apply_gain(14, 1, 256, 512)
+        apply_gain(15, 1, 256, 512)
+        quantize_result(3, 1, 0, 256)
+        interleave(3, 1, 256, 512)
+        quantize_result(3, 1, 256, 512)
         store_scales(slice(3, 4), [nc.scalar, nc.sync])

from contextlib import ExitStack

import concourse.mybir as mybir
from concourse.masks import make_identity

F32 = mybir.dt.float32
BF16 = mybir.dt.bfloat16
U32 = mybir.dt.uint32
I32 = mybir.dt.int32
U8 = mybir.dt.uint8
FP8X4 = mybir.dt.float8_e4m3fn_x4
ACT = mybir.ActivationFunctionType
ALU = mybir.AluOpType

ITEMS, USERS = 2048, 1024
FLOPS = 2 * ITEMS * ITEMS * USERS
P = 128
PASSES = 4
H, C = "history", "cooc"


def T(kind, *ns):
    return [("T", kind, n) for n in ns]


def M(n, half, lo=0, hi=512):
    return [("M", n, half, lo, hi)]


def tail(widths):
    out, lo = [], 0
    for w in widths:
        out += M(14, 1, lo, lo + w) + M(15, 1, lo, lo + w)
        lo += w
    return out


TAIL = []
RAW, REG, GR, YB = 12, 4, 4, 4
A_ON_VECTOR = set()
GAIN_ON_SCALAR = set()
LF, LB, LD, LE, LQ = 2, 1, 2, 0, 1


def tile_cooccurrence_history_log_scores_g2_kernel(tc, cooc, history, damp, gain, out_0, out_1, out_2):
    nc = tc.nc
    PLAN = (T(H,0,1)+T(C,0,1)+T(H,2,3)+M(0,0,0,256)+M(1,0,0,256)+T(C,2,3)+M(0,0,256,512)+M(1,0,256,512)+T(H,4,5)+M(2,0)+M(3,0)+T(H,6,7)+M(0,1,0,256)+M(1,1,0,256)+M(2,1,0,256)+M(3,1,0,256)+T(C,4,5)+M(0,1,256,512)+M(1,1,256,512)+M(2,1,256,512)+M(3,1,256,512)+T(C,6,7)+M(4,0)+M(5,0)+M(4,1)+M(5,1)+T(C,8,9)+M(6,0)+M(7,0)+M(6,1)+M(7,1)+T(C,10,11)+M(8,0)+M(9,0)+M(8,1)+M(9,1)+T(C,12,13)+M(10,0)+M(11,0)+M(10,1)+M(11,1)+T(C,14,15)+M(12,0)+M(13,0)+M(14,0)+M(15,0)+M(12,1)+M(13,1)) + tail(TAIL)
    cooc_rows = cooc.rearrange("(g m t) k -> g t m k", m=P, t=4)
    hist_rows = history.rearrange("(r p) k -> r p k", p=P)
    chunks = [(s[1], s[2]) for s in PLAN if s[0] == "T"]

    with ExitStack() as ctx:
        sb = ctx.enter_context(tc.tile_pool(name="sb", bufs=1))
        ps = ctx.enter_context(tc.psum_pool(name="ps", bufs=1))
        ctx.enter_context(tc.manual_schedule())

        def tiles(pool, n, name, shape, dtype):
            if pool is ps:
                return [pool.tile(shape, dtype, name="%s%d" % (name, i)) for i in range(n)]
            return [pool.tile(shape, dtype, name="%s%d" % (name, i), align_bytes=64) for i in range(n)]

        raw = tiles(sb, RAW, "raw", [P, ITEMS], BF16)
        regrouped = tiles(sb, REG, "reg", [P, 2, ITEMS // 2], BF16)
        grouped = tiles(sb, GR, "grp", [P, PASSES, 512], BF16)
        h_grouped = tiles(sb, 2, "hgrp", [P, PASSES, 2, 512], BF16)
        h_codes = tiles(sb, 2, "hc", [P, PASSES, 512], U32)
        h_scales = tiles(sb, 2, "hs", [P, PASSES, 512], U8)
        c_codes = tiles(sb, 16, "cc", [P, PASSES, P], U32)
        c_scales = tiles(sb, 16, "cs", [P, PASSES, P], U8)
        y = tiles(sb, YB, "y", [P, 4, 512], F32)
        y_bf = tiles(sb, 2, "ybf", [P, 512, 4], BF16)
        y_codes = tiles(sb, 3, "yc", [P, 512], U32)
        y_scales = sb.tile([P, 4, USERS], U8, name="ys", align_bytes=64)
        ident = sb.tile([P, P], F32, name="ident", align_bytes=64)
        damp_bf = sb.tile([P, 4, 4], BF16, name="damp_bf", align_bytes=64)
        gain_bf = sb.tile([P, 4, 4], BF16, name="gain_bf", align_bytes=64)
        damp_f = sb.tile([P, 16], F32, name="damp_f", align_bytes=64)
        gain_f = sb.tile([P, 16], F32, name="gain_f", align_bytes=64)
        warm = sb.tile([P, 1], F32, name="warm", align_bytes=64)
        t_banks = tiles(ps, 4, "tb", [P, 2, 2, P], F32)
        m_banks = tiles(ps, 4, "mb", [P, 512], F32)

        make_identity(nc, ident[:])
        nc.scalar.activation(out=warm[:], in_=ident[:, 0:1], func=ACT.Ln, bias=1.0, scale=1.0)

        def load(j):
            kind, r = chunks[j]
            src = hist_rows[r] if kind == H else cooc_rows[r // 4, r % 4]
            nc.sync.dma_start(out=raw[j % RAW][:], in_=src)
            if j == 7:
                nc.sync.dma_start(out=damp_bf[:], in_=damp.rearrange("(g p t) -> p g t", p=P, t=4))
                nc.gpsimd.tensor_copy(out=damp_f[:], in_=damp_bf[:].rearrange("p g t -> p (g t)"))
            if j == 7:
                nc.sync.dma_start(out=gain_bf[:], in_=gain.rearrange("(g p t) -> p g t", p=P, t=4))
                nc.gpsimd.tensor_copy(out=gain_f[:], in_=gain_bf[:].rearrange("p g t -> p (g t)"))

        def regroup(j):
            if j not in set(range(6)):
                nc.vector.tensor_copy(
                    out=regrouped[j % REG][:].bitcast(F32).rearrange("p u w -> p w u"),
                    in_=raw[j % RAW][:].bitcast(F32).rearrange("p (w u) -> p w u", u=2),
                )

        def transpose(j):
            if j in set(range(6)):
                words = raw[j % RAW][:].bitcast(F32).rearrange("p (w u) -> p u w", u=2)
            else:
                words = regrouped[j % REG][:].bitcast(F32)
            for b in range(2):
                bank = t_banks[2 * (j % 2) + b]
                for a in range(2):
                    kp = 2 * b + a
                    for u in range(2):
                        nc.tensor.transpose(bank[:, a, u, :], words[:, u, kp * P:(kp + 1) * P], ident[:])
                kind, n = chunks[j]
                if kind == H:
                    dst = h_grouped[(n // 2) % 2][:, 2 * b:2 * b + 2, n % 2, :]
                else:
                    dst = grouped[n % GR][:, 2 * b:2 * b + 2, :]
                dst = dst.bitcast(F32).rearrange("p a (r u) -> p a r u", u=2)
                src = bank[:].rearrange("p a u r -> p a r u")
                if (j, b) in A_ON_VECTOR:
                    nc.vector.tensor_copy(out=dst, in_=src)
                else:
                    nc.scalar.copy(out=dst, in_=src)

        def quantize_operand(j):
            kind, n = chunks[j]
            if kind == C:
                nc.vector.quantize_mx(
                    out=c_codes[n][:].rearrange("p a b -> p (a b)").bitcast(FP8X4),
                    scales=c_scales[n][:].rearrange("p a b -> p (a b)"),
                    in_=grouped[n % GR][:].rearrange("p a b -> p (a b)"),
                )
            elif n % 2 == 1:
                cols = slice(P * (n % 4 - 1), P * (n % 4 + 1))
                for kp in range(PASSES):
                    nc.vector.quantize_mx(
                        out=h_codes[n // 4][:, kp, cols].bitcast(FP8X4),
                        scales=h_scales[n // 4][:, kp, cols],
                        in_=h_grouped[(n // 2) % 2][:, kp, :, :].rearrange("p c w -> p (c w)"),
                    )

        y_slot = {}

        def multiply(bank, n, half, lo, hi):
            g, t = n // 4, n % 4
            yt = y[y_slot.setdefault((g, half), len(y_slot)) % YB]
            acc = m_banks[bank % 4]
            for kp in range(PASSES):
                nc.tensor.matmul_mx(
                    out=acc[:, 0:hi - lo],
                    lhsT=c_codes[n][:, kp, :].bitcast(FP8X4),
                    lhsT_scale=c_scales[n][:, kp, :],
                    rhs=h_codes[half][:, kp, lo:hi].bitcast(FP8X4),
                    rhs_scale=h_scales[half][:, kp, lo:hi],
                    start=(kp == 0),
                    stop=(kp == PASSES - 1),
                )
            nc.scalar.activation(out=yt[:, t, lo:hi], in_=acc[:, 0:hi - lo], func=ACT.Ln, bias=1.0, scale=damp_f[:, n:n + 1])

        def store_y(g, half, ts, lo, hi):
            yt = y[y_slot[(g, half)] % YB]
            rows = out_0[512 * g:512 * g + 512, 512 * half + lo:512 * half + hi].rearrange("(p t) m -> p t m", t=4)
            nc.sync.dma_start(out=rows[:, ts, :], in_=yt[:, ts, lo:hi])

        def apply_gain(n, half, lo, hi):
            g, t = n // 4, n % 4
            yt = y[y_slot[(g, half)] % YB]
            if (n, half) in GAIN_ON_SCALAR:
                nc.scalar.activation(out=yt[:, t, lo:hi], in_=yt[:, t, lo:hi], func=ACT.Copy, scale=gain_f[:, n:n + 1])
            else:
                nc.vector.tensor_scalar(out=yt[:, t, lo:hi], in0=yt[:, t, lo:hi], scalar1=gain_f[:, n:n + 1], scalar2=None, op0=ALU.mult)
            if g == 3 and t == 1:
                store_y(g, half, slice(0, 2), 0, 512)
            elif g == 3 and t == 3:
                store_y(g, half, slice(2, 4), lo, hi)
            elif t == 3 and hi == 512:
                store_y(g, half, slice(0, 4), 0, 512)

        def interleave(g, half, lo, hi):
            s = y_slot[(g, half)]
            (nc.scalar.copy if (g, half, lo) in set() else nc.vector.tensor_copy)(
                out=y_bf[s % 2][:, lo:hi, :].rearrange("p (c i) t -> p c t i", i=4),
                in_=y[s % YB][:, :, lo:hi].rearrange("p t (c i) -> p c t i", i=4),
            )

        def store_scales(gs, engines):
            for q in range(4):
                engines[q % len(engines)].dma_start(
                    out=out_2[gs, 4 * q:4 * q + 4, :].rearrange("g r m -> r g m").bitcast(I32),
                    in_=y_scales[32 * q:32 * q + 4, gs, :].bitcast(I32),
                )

        def quantize_result(g, half, lo, hi):
            s = y_slot[(g, half)]
            users = slice(512 * half + lo, 512 * half + hi)
            nc.vector.quantize_mx(
                out=y_codes[s % 3][:, lo:hi].bitcast(FP8X4),
                scales=y_scales[:, g, users],
                in_=y_bf[s % 2][:, lo:hi, :].rearrange("p m t -> p (m t)"),
            )
            nc.sync.dma_start(
                out=out_1[g, :, users, :].rearrange("p m t -> p (m t)").bitcast(I32),
                in_=y_codes[s % 3][:, lo:hi].bitcast(I32),
            )
            if (g, half) == (2, 1):
                store_scales(slice(0, 3), [nc.sync])

        for j in range(RAW):
            load(j)
        for j in range(LF):
            regroup(j)
        later = {}

        def after(step, rank, fn, *args):
            later.setdefault(step, []).append((rank, len(later.get(step, [])), fn, args))

        j = 0
        bank = 0
        needs = {}
        for si, step in enumerate(PLAN):
            if step[0] == "M":
                needs.setdefault((C, step[1]), si)
                for r in range(4 * step[2] + step[3] // P, 4 * step[2] + step[4] // P):
                    needs.setdefault((H, r), si)
        for si, step in enumerate(PLAN):
            if step[0] == "T":
                transpose(j)
                if j + RAW < len(chunks):
                    load(j + RAW)
                if j + LF < len(chunks):
                    after(si, 3 if j + LF < 8 else 1, regroup, j + LF)
                after(min(si + LB, needs[chunks[j]] - 1), 2, quantize_operand, j)
                j += 1
            else:
                n, half, lo, hi = step[1:]
                multiply(bank, n, half, lo, hi)
                bank += 1
                ld = LD if n < 12 else 1
                after(si + (1 if (n, half) in GAIN_ON_SCALAR else ld), 0, apply_gain, n, half, lo, hi)
                if n % 4 == 3 and (hi == 512 or (n, half) == (15, 1)):
                    if (n, half) != (15, 1):
                        lo = 0
                    le = LE if n < 15 else 0
                    after(si + ld + le, 3, interleave, n // 4, half, lo, hi)
                    after(si + ld + le + LQ, 4, quantize_result, n // 4, half, lo, hi)
            for rank, order, fn, args in sorted(later.get(si, []), key=lambda x: x[:2]):
                fn(*args)
        def flush(si):
            for rank, order, fn, args in sorted(later.get(si, []), key=lambda x: x[:2]):
                fn(*args)

        multiply(bank, 14, 1, 0, 256)
        flush(len(PLAN))
        flush(len(PLAN) + 1)
        multiply(bank + 1, 15, 1, 0, 256)
        apply_gain(14, 1, 0, 256)
        apply_gain(15, 1, 0, 256)
        multiply(bank + 2, 14, 1, 256, 512)
        interleave(3, 1, 0, 256)
        multiply(bank + 3, 15, 1, 256, 512)
        apply_gain(14, 1, 256, 512)
        apply_gain(15, 1, 256, 512)
        quantize_result(3, 1, 0, 256)
        interleave(3, 1, 256, 512)
        quantize_result(3, 1, 256, 512)
        store_scales(slice(3, 4), [nc.scalar, nc.sync])
